import numpy as np, ml_dtypes
CORES = [2,6,10,14,18,22,26,30,34,38,42,46,50,54,58,62]
N = 16
T = 24
ROUTE = [[[5,13],[13,9],[15,6],[15,5],[7,0],[0,11],[13,2],[4,7],[7,1],[13,14],[1,10],[15,3],[11,0],[4,2],[3,0],[14,5],[10,12],[15,4],[5,1],[15,7],[2,6],[6,2],[3,15],[12,6]],[[10,4],[13,9],[11,14],[12,10],[15,12],[8,0],[2,5],[15,0],[15,2],[7,10],[3,5],[5,11],[10,11],[9,7],[3,5],[2,5],[13,11],[5,1],[7,13],[5,0],[11,15],[12,7],[7,5],[2,14]],[[13,15],[1,9],[1,8],[9,1],[13,7],[5,12],[2,10],[4,15],[1,8],[4,15],[0,6],[11,4],[11,13],[15,9],[4,8],[4,0],[12,4],[0,8],[10,7],[13,8],[12,4],[4,3],[12,3],[5,0]],[[14,4],[2,3],[9,4],[9,10],[12,15],[7,5],[5,12],[6,1],[1,0],[12,14],[2,12],[5,7],[8,10],[1,7],[12,4],[9,15],[3,1],[10,9],[9,6],[2,10],[6,11],[2,10],[13,3],[2,14]],[[0,14],[15,12],[12,2],[7,0],[1,13],[1,7],[8,12],[13,14],[7,12],[12,10],[15,7],[2,1],[15,5],[15,11],[6,14],[8,7],[15,12],[9,12],[0,5],[10,6],[9,12],[4,2],[5,2],[9,12]],[[14,3],[5,13],[6,10],[11,6],[8,2],[0,10],[8,4],[6,7],[8,12],[5,12],[14,12],[13,14],[8,5],[12,8],[3,6],[6,1],[11,0],[2,1],[12,14],[14,7],[0,4],[3,9],[6,14],[11,0]],[[11,5],[4,13],[1,9],[6,13],[12,7],[7,14],[0,2],[2,13],[6,4],[1,15],[15,10],[4,8],[4,11],[9,0],[2,5],[3,6],[11,8],[11,1],[5,1],[15,8],[12,5],[1,3],[7,11],[8,13]],[[6,13],[2,10],[7,6],[1,11],[5,0],[11,15],[15,5],[14,0],[8,1],[6,3],[9,12],[6,14],[11,0],[11,5],[8,0],[12,5],[5,13],[6,7],[9,14],[11,2],[7,12],[5,11],[11,4],[0,13]],[[0,6],[3,6],[11,9],[3,5],[7,13],[14,15],[6,8],[5,13],[12,7],[15,8],[1,14],[6,1],[10,14],[9,4],[7,5],[12,4],[12,1],[0,9],[14,6],[15,7],[15,1],[0,11],[4,15],[10,14]],[[11,12],[14,2],[8,3],[11,8],[14,3],[6,10],[2,9],[7,4],[4,8],[3,9],[6,4],[15,6],[1,10],[11,0],[6,4],[9,1],[8,13],[1,3],[0,7],[14,15],[11,13],[0,11],[4,11],[12,14]],[[14,7],[14,7],[0,14],[7,2],[11,15],[4,5],[0,8],[10,9],[6,1],[14,5],[6,4],[0,5],[4,7],[3,5],[3,12],[3,6],[6,0],[2,7],[7,3],[7,6],[13,0],[12,9],[10,11],[13,1]],[[15,1],[12,15],[5,1],[2,8],[15,8],[5,9],[10,11],[15,8],[12,9],[1,3],[9,2],[15,10],[4,9],[9,12],[3,8],[14,7],[1,11],[13,3],[15,6],[11,6],[1,15],[9,10],[13,5],[0,13]],[[6,5],[1,6],[6,5],[10,0],[7,14],[7,11],[12,6],[8,5],[11,15],[4,10],[11,4],[9,2],[1,7],[9,10],[12,5],[12,0],[8,6],[7,3],[0,6],[12,6],[15,6],[5,13],[12,9],[4,12]],[[1,4],[0,2],[5,14],[3,15],[1,2],[10,3],[5,9],[14,9],[13,12],[3,8],[11,0],[13,8],[14,10],[8,11],[4,11],[11,6],[5,2],[8,5],[0,10],[1,5],[11,6],[0,1],[0,5],[10,7]],[[4,10],[5,6],[3,5],[9,13],[8,10],[6,12],[12,9],[1,7],[9,10],[7,9],[13,6],[2,14],[14,5],[5,14],[1,12],[15,2],[15,5],[3,0],[0,9],[4,0],[2,14],[2,13],[11,12],[14,15]],[[8,5],[9,7],[9,2],[4,5],[13,10],[8,11],[12,3],[11,1],[2,6],[7,14],[10,15],[9,7],[15,8],[6,10],[10,15],[13,7],[8,6],[5,3],[5,8],[15,13],[8,7],[8,2],[3,9],[2,6]]]
YW = 63
def setup_inputs(rng):
    return {"x": rng.standard_normal((N, 128, T), dtype=np.float32).astype(ml_dtypes.bfloat16)}
def reference(x):
    y = np.full((N, 128, YW), np.nan, x.dtype)
    fill = [0] * N
    for r in range(N):
        for t in range(T):
            for e in ROUTE[r][t]:
                y[e][:, fill[e]] = x[r][:, t]
                fill[e] += 1
    return {"y": y}

@@ -1,0 +1,151 @@
+import concourse.bass as bass
+
+P = 128
+NSLOT = 16
+SCRATCH = {
+    "xin": ("sbuf", [P, NSLOT * 24], "bfloat16"),
+    "land": ("sbuf", [P, 64], "bfloat16"),
+}
+SEMAPHORES = ["ld", "xarr", "carr", "sent", "st"]
+
+PLANS = {}
+
+
+def pack_chip(n, nranks, a, b, cap):
+    items = sorted([r for r in range(nranks) if r not in (a, b)], key=lambda r: -(n[r][a] + n[r][b]))
+    load = [0] * 6
+    rk = [n[a][b] + n[b][b], n[a][a] + n[b][a]]
+    if max(rk) > cap:
+        return None
+    cur = {}
+    nodes = [0]
+
+    def dfs(i):
+        nodes[0] += 1
+        if nodes[0] > 50000:
+            return False
+        if i == len(items):
+            return True
+        r = items[i]
+        s = n[r][a] + n[r][b]
+        seen = set()
+        for h in sorted(range(6), key=lambda k: load[k]):
+            if load[h] in seen or load[h] + s > cap:
+                continue
+            seen.add(load[h])
+            load[h] += s
+            cur[r] = h
+            if dfs(i + 1):
+                return True
+            load[h] -= s
+        if (n[r][a] == 0 or n[r][b] == 0) and rk[0] + n[r][b] <= cap and rk[1] + n[r][a] <= cap:
+            rk[0] += n[r][b]
+            rk[1] += n[r][a]
+            cur[r] = -1
+            if dfs(i + 1):
+                return True
+            rk[0] -= n[r][b]
+            rk[1] -= n[r][a]
+        cur.pop(r, None)
+        return False
+
+    return dict(cur) if dfs(0) else None
+
+
+def make_plan(route, cores, ntok):
+    nranks = len(cores)
+    n = [[0] * nranks for r in range(nranks)]
+    cols = [[] for r in range(nranks)]
+    for r in range(nranks):
+        for t in range(ntok):
+            for e in route[r][t]:
+                n[r][e] += 1
+                cols[e].append((r, t))
+    work = {}
+    for c in range(nranks // 2):
+        a, b = 2 * c, 2 * c + 1
+        base = (cores[a] // 8) * 8
+        helpers = [base + k for k in range(8) if base + k not in (cores[a], cores[b])]
+        got = None
+        for cap in range(8, 17):
+            got = pack_chip(n, nranks, a, b, cap)
+            if got is not None:
+                break
+        where = {}
+        if got is None:
+            load = {w: 0 for w in helpers + [cores[a], cores[b]]}
+            for r in range(nranks):
+                for e in (a, b):
+                    w = min([k for k in load if k != cores[e]], key=lambda k: load[k])
+                    where[(r, e)] = w
+                    load[w] += n[r][e]
+        else:
+            for r in range(nranks):
+                h = got.get(r, -1)
+                where[(r, a)] = helpers[h] if h >= 0 else cores[b]
+                where[(r, b)] = helpers[h] if h >= 0 else cores[a]
+        for e in (a, b):
+            for pos, (r, t) in enumerate(cols[e]):
+                work.setdefault(where[(r, e)], []).append((r, t, e, pos))
+    deliver = [[] for r in range(nranks)]
+    for w in sorted(work):
+        for r in sorted(set(k[0] for k in work[w])):
+            if cores[r] != w:
+                deliver[r].append(w)
+    return work, deliver, [len(k) for k in cols]
+
+
+def rank_program(g, core, T, topo):
+    ntok = T.tables["T"]
+    cores = list(T.cores)
+    if "plan" not in PLANS:
+        PLANS["plan"] = make_plan(T.tables["ROUTE"], cores, ntok)
+    work, deliver, count = PLANS["plan"]
+    rank = T.rank_of(core)
+    sem = T.sem
+    sent = 0
+
+    def dst_id(c):
+        rid, pid, se = topo.addr(c)
+        return bass.DstId(rid=rid, pnc=pid)
+
+    def hops(c):
+        a, b = topo.chip(core), topo.chip(c)
+        return 0 if a == b else 1 if (topo.mates(a, b) or topo.same_plane(a, b)) else 2
+
+    if rank is not None:
+        blk = T.xin[:, rank * ntok:(rank + 1) * ntok]
+        g.dma_start(blk, T.x[:, :]).then_inc(sem.ld, 16)
+        g.wait_ge(sem.ld, 16)
+        far = sorted([c for c in deliver[rank] if hops(c) > 0], key=lambda c: -hops(c))
+        near = [c for c in deliver[rank] if hops(c) == 0]
+        trs = []
+        for dsts, mask in ((far, 0x00FF), (near, 0xFF00)):
+            if dsts:
+                trs.append(bass.RemoteDMATransfer(dst_ids=[dst_id(c) for c in dsts], dma_engine_mask=mask,
+                                                  remote_sem=sem.xarr, srcs=[blk], dsts=[blk for c in dsts]))
+                sent += 8
+        if trs:
+            g.remote_dma_fused(trs, local_sem=sem.sent)
+
+    mine = work.get(core, [])
+    nblk = sum(1 for r in range(len(cores)) if core in deliver[r])
+    if nblk:
+        g.wait_ge(sem.xarr, 8 * nblk)
+    for i in range(0, len(mine), 16):
+        part = mine[i:i + 16]
+        trs = []
+        for k, (r, t, e, pos) in enumerate(part):
+            trs.append(bass.RemoteDMATransfer(dst_ids=[dst_id(cores[e])], dma_engine_mask=1 << k, remote_sem=sem.carr,
+                                              srcs=[T.xin[:, r * ntok + t:r * ntok + t + 1]],
+                                              dsts=[T.land[:, pos:pos + 1]]))
+            sent += 1
+        g.remote_dma_fused(trs, local_sem=sem.sent)
+
+    if rank is not None:
+        g.wait_ge(sem.carr, count[rank])
+        g.dma_start(T.y[:, 0:count[rank]], T.land[:, 0:count[rank]]).then_inc(sem.st, 16)
+    if sent:
+        g.wait_ge(sem.sent, sent)
+    if rank is not None:
+        g.wait_ge(sem.st, 16)

@@ -117,7 +117,8 @@ def rank_program(g, core, T, topo):
         blk = T.xin[:, rank * ntok:(rank + 1) * ntok]
         g.dma_start(blk, T.x[:, :]).then_inc(sem.ld, 16)
         g.wait_ge(sem.ld, 16)
-        far = sorted([c for c in deliver[rank] if hops(c) > 0], key=lambda c: -hops(c))
+        far = sorted([c for c in deliver[rank] if hops(c) > 0],
+                     key=lambda c: (-hops(c), (topo.chip(c) ^ topo.chip(core)) >> 1))
         near = [c for c in deliver[rank] if hops(c) == 0]
         trs = []
         for dsts, mask in ((far, 0x00FF), (near, 0xFF00)):

import concourse.bass as bass

P = 128
NSLOT = 16
SCRATCH = {
    "xin": ("sbuf", [P, NSLOT * 24], "bfloat16"),
    "land": ("sbuf", [P, 64], "bfloat16"),
}
SEMAPHORES = ["ld", "xarr", "carr", "sent", "st"]

PLANS = {}


def pack_chip(n, nranks, a, b, cap):
    items = sorted([r for r in range(nranks) if r not in (a, b)], key=lambda r: -(n[r][a] + n[r][b]))
    load = [0] * 6
    rk = [n[a][b] + n[b][b], n[a][a] + n[b][a]]
    if max(rk) > cap:
        return None
    cur = {}
    nodes = [0]

    def dfs(i):
        nodes[0] += 1
        if nodes[0] > 50000:
            return False
        if i == len(items):
            return True
        r = items[i]
        s = n[r][a] + n[r][b]
        seen = set()
        for h in sorted(range(6), key=lambda k: load[k]):
            if load[h] in seen or load[h] + s > cap:
                continue
            seen.add(load[h])
            load[h] += s
            cur[r] = h
            if dfs(i + 1):
                return True
            load[h] -= s
        if (n[r][a] == 0 or n[r][b] == 0) and rk[0] + n[r][b] <= cap and rk[1] + n[r][a] <= cap:
            rk[0] += n[r][b]
            rk[1] += n[r][a]
            cur[r] = -1
            if dfs(i + 1):
                return True
            rk[0] -= n[r][b]
            rk[1] -= n[r][a]
        cur.pop(r, None)
        return False

    return dict(cur) if dfs(0) else None


def make_plan(route, cores, ntok):
    nranks = len(cores)
    n = [[0] * nranks for r in range(nranks)]
    cols = [[] for r in range(nranks)]
    for r in range(nranks):
        for t in range(ntok):
            for e in route[r][t]:
                n[r][e] += 1
                cols[e].append((r, t))
    work = {}
    for c in range(nranks // 2):
        a, b = 2 * c, 2 * c + 1
        base = (cores[a] // 8) * 8
        helpers = [base + k for k in range(8) if base + k not in (cores[a], cores[b])]
        got = None
        for cap in range(8, 17):
            got = pack_chip(n, nranks, a, b, cap)
            if got is not None:
                break
        where = {}
        if got is None:
            load = {w: 0 for w in helpers + [cores[a], cores[b]]}
            for r in range(nranks):
                for e in (a, b):
                    w = min([k for k in load if k != cores[e]], key=lambda k: load[k])
                    where[(r, e)] = w
                    load[w] += n[r][e]
        else:
            for r in range(nranks):
                h = got.get(r, -1)
                where[(r, a)] = helpers[h] if h >= 0 else cores[b]
                where[(r, b)] = helpers[h] if h >= 0 else cores[a]
        for e in (a, b):
            for pos, (r, t) in enumerate(cols[e]):
                work.setdefault(where[(r, e)], []).append((r, t, e, pos))
    deliver = [[] for r in range(nranks)]
    for w in sorted(work):
        for r in sorted(set(k[0] for k in work[w])):
            if cores[r] != w:
                deliver[r].append(w)
    return work, deliver, [len(k) for k in cols]


def rank_program(g, core, T, topo):
    ntok = T.tables["T"]
    cores = list(T.cores)
    if "plan" not in PLANS:
        PLANS["plan"] = make_plan(T.tables["ROUTE"], cores, ntok)
    work, deliver, count = PLANS["plan"]
    rank = T.rank_of(core)
    sem = T.sem
    sent = 0

    def dst_id(c):
        rid, pid, se = topo.addr(c)
        return bass.DstId(rid=rid, pnc=pid)

    def hops(c):
        a, b = topo.chip(core), topo.chip(c)
        return 0 if a == b else 1 if (topo.mates(a, b) or topo.same_plane(a, b)) else 2

    if rank is not None:
        blk = T.xin[:, rank * ntok:(rank + 1) * ntok]
        g.dma_start(blk, T.x[:, :]).then_inc(sem.ld, 16)
        g.wait_ge(sem.ld, 16)
        far = sorted([c for c in deliver[rank] if hops(c) > 0],
                     key=lambda c: (-hops(c), (topo.chip(c) ^ topo.chip(core)) >> 1))
        near = [c for c in deliver[rank] if hops(c) == 0]
        trs = []
        for dsts, mask in ((far, 0x00FF), (near, 0xFF00)):
            if dsts:
                trs.append(bass.RemoteDMATransfer(dst_ids=[dst_id(c) for c in dsts], dma_engine_mask=mask,
                                                  remote_sem=sem.xarr, srcs=[blk], dsts=[blk for c in dsts]))
                sent += 8
        if trs:
            g.remote_dma_fused(trs, local_sem=sem.sent)

    mine = work.get(core, [])
    nblk = sum(1 for r in range(len(cores)) if core in deliver[r])
    if nblk:
        g.wait_ge(sem.xarr, 8 * nblk)
    for i in range(0, len(mine), 16):
        part = mine[i:i + 16]
        trs = []
        for k, (r, t, e, pos) in enumerate(part):
            trs.append(bass.RemoteDMATransfer(dst_ids=[dst_id(cores[e])], dma_engine_mask=1 << k, remote_sem=sem.carr,
                                              srcs=[T.xin[:, r * ntok + t:r * ntok + t + 1]],
                                              dsts=[T.land[:, pos:pos + 1]]))
            sent += 1
        g.remote_dma_fused(trs, local_sem=sem.sent)

    if rank is not None:
        g.wait_ge(sem.carr, count[rank])
        g.dma_start(T.y[:, 0:count[rank]], T.land[:, 0:count[rank]]).then_inc(sem.st, 16)
    if sent:
        g.wait_ge(sem.sent, sent)
    if rank is not None:
        g.wait_ge(sem.st, 16)
